import numpy as np
import ml_dtypes


def mxq(x, axis, fmt="e4m3"):
    dtype, down = {"e4m3": (ml_dtypes.float8_e4m3fn, 7), "e5m2": (ml_dtypes.float8_e5m2, 14)}[fmt]
    v = np.moveaxis(np.asarray(x, np.float32).astype(ml_dtypes.bfloat16).astype(np.float64), axis, -1)
    blocks = v.reshape(v.shape[:-1] + (-1, 32))
    amax = np.abs(blocks).max(-1, keepdims=True)
    byte = np.maximum(np.where(amax > 0, np.frexp(amax)[1] - 1 + 127, 0) - down, 1)
    scale = np.exp2(byte - 127.0)
    codes = (blocks / scale).astype(np.float32).astype(dtype).astype(np.float64)
    return np.moveaxis((codes * scale).reshape(v.shape), -1, axis)


WIDE = False


def mx_kscale(k):
    if not WIDE:
        return np.ones(k)
    levels = np.array([10, -10, 5, -5, 0])
    if k % 512:
        return np.exp2(np.random.permutation(np.resize(levels, k // 32))).repeat(32)
    a = np.empty((k // 512, 16))
    for p in range(k // 512):
        a[p, :8] = np.random.permutation(np.resize(levels, 8))
        for g in range(8):
            far = levels[np.abs(levels - a[p, g]) >= 10]
            a[p, g + 8] = far[np.random.randint(len(far))]
    return np.exp2(a.ravel()).repeat(32)


def f64(x):
    return np.asarray(x).astype(np.float64)


def striped(idx):
    return np.tile(idx.reshape(-1, 16).T, (8, 1)).astype(np.uint16)


def unstriped(offs):
    return offs[:16].T.reshape(-1).astype(np.int64)


def gelu(v):
    return 0.5 * v * (1.0 + np.tanh(np.sqrt(2.0 / np.pi) * (v + 0.044715 * v**3)))


K, T, E, C, N = 1024, 1536, 8, 128, 128


def by_expert(wq, xq):
    return np.concatenate([wq[e].T @ xq[:, e * C:(e + 1) * C] for e in range(E)], axis=1)


def setup_inputs():
    n = np.random.standard_normal
    s = mx_kscale(K)[:, None]
    return {
        "xT": (n((K, T)) * s).astype(np.float32),
        "w": (n((E + 1, K, N)) / np.sqrt(K) / s[None]).astype(np.float32),
        "b": (0.3 * n((N, E + 1))).astype(np.float32),
        "gate": np.tile(np.random.uniform(0.2, 1.0, E * C), (N, 1)).astype(np.float32),
        "offs": striped(np.random.permutation(T)[:E * C]),
    }


def reference(xT, w, b, gate, offs):
    idx = unstriped(offs)
    wq = mxq(f64(w), 1, "e4m3")
    xs = mxq(f64(xT), 0, "e4m3")
    ys = gelu((wq[E].T @ xs) + f64(b)[:, E:])
    xq = mxq(f64(xT)[:, idx], 0, "e4m3")
    y = by_expert(wq, xq)
    y = gelu(y + np.repeat(f64(b)[:, :E], C, axis=1))
    out = ys
    out[:, idx] += f64(gate) * y
    return out

@@ -1,0 +1,179 @@
+import concourse.mybir as mybir
+
+F32 = mybir.dt.float32
+BF16 = mybir.dt.bfloat16
+U32 = mybir.dt.uint32
+I32 = mybir.dt.int32
+U16 = mybir.dt.uint16
+U8 = mybir.dt.uint8
+FP8X4 = mybir.dt.float8_e4m3fn_x4
+GELU = mybir.ActivationFunctionType.Gelu_apprx_tanh
+MULT = mybir.AluOpType.mult
+
+P = 128
+K, T, E, C, N = 1024, 1536, 8, 128, 128
+S = E * C
+FLOPS = 2 * K * N * (T + S)
+PASSES = 2
+TC = 512
+
+X_ON_VECTOR = {(0, 0, 0), (0, 0, 1), (0, 1, 0), (0, 1, 1)}
+W_ON_VECTOR = {8}
+XI_ON_SCALAR = {(1, 2)}
+
+
+def tile_moe_shr_lin_gelu_kernel(tc, xT, w, b, gate, offs, out):
+    nc = tc.nc
+
+    def vcopy(o, i):
+        nc.vector.tensor_copy(out=o, in_=i)
+
+    def scopy(o, i):
+        nc.scalar.copy(out=o, in_=i)
+
+    with (
+        tc.tile_pool(name="keep", bufs=1) as keep,
+        tc.psum_pool(name="psum", bufs=1) as psum,
+    ):
+        offsets = keep.tile([P, S // 16], U16, name="offsets")
+        bias = keep.tile([P, E + 1], F32, name="bias")
+        gates = keep.tile([P, S], F32, name="gates")
+        xs = [[keep.tile([P, 2, T], F32, name=f"xs{c}{u}") for u in range(2)] for c in range(2)]
+        xp = [keep.tile([P, 2, 2 * T], BF16, name=f"xp{c}", align_bytes=64) for c in range(2)]
+        xi = [keep.tile([P, 4 * T], BF16, name=f"xi{c}", align_bytes=64) for c in range(2)]
+        xg = keep.tile([P, 2, S], U32, name="xg", align_bytes=64)
+        gi = [keep.tile([P, 4 * S], BF16, name=f"gi{c}", align_bytes=64) for c in range(2)]
+        xq = [keep.tile([P, T], U32, name=f"xq{c}", align_bytes=64) for c in range(2)]
+        xsc = [keep.tile([P, T], U8, name=f"xsc{c}", align_bytes=64) for c in range(2)]
+        gq = [keep.tile([P, S], U32, name=f"gq{c}", align_bytes=64) for c in range(2)]
+        gsc = [keep.tile([P, S], U8, name=f"gsc{c}", align_bytes=64) for c in range(2)]
+        groups = [(8,), (0, 1), (2, 3), (4, 5), (6, 7)]
+        ws = {}
+        wb = {}
+        wq = {}
+        wsc = {}
+        for g in groups:
+            n = len(g) * 2
+            ws[g] = keep.tile([P, n, 512], F32, name=f"ws{g[0]}")
+            wb[g] = keep.tile([P, n * 512], BF16, name=f"wb{g[0]}", align_bytes=64)
+            wq[g] = keep.tile([P, n * 128], U32, name=f"wq{g[0]}", align_bytes=64)
+            wsc[g] = keep.tile([P, n * 128], U8, name=f"wsc{g[0]}", align_bytes=64)
+        ys = keep.tile([P, T], F32, name="ys")
+        y = keep.tile([P, S], F32, name="y")
+        z = keep.tile([P, T], F32, name="z")
+        dummy = keep.tile([P, 8], F32, name="dummy")
+        ps = [psum.tile([P, TC], F32, name=f"ps{i}") for i in range(3)]
+        pr = [psum.tile([P, 2 * N], F32, name=f"pr{i}") for i in range(4)]
+
+        nc.vector.memset(dummy[:], 0.0)
+        nc.scalar.activation(out=dummy[:, 4:5], in_=dummy[:, 0:1], func=GELU)
+        nc.gpsimd.memset(z[:], 0.0)
+
+        def load_x(c, u, cols):
+            rows = xT[c * 512 : (c + 1) * 512, cols].rearrange("(p u j) t -> p u j t", u=2, j=2)
+            nc.sync.dma_start(out=xs[c][u][:, :, cols], in_=rows[:, u])
+
+        for i in range(3):
+            load_x(0, 0, slice(i * 512, (i + 1) * 512))
+        nc.sync.dma_start(offsets[:], offs)
+        for c, u in ((0, 1), (1, 0), (1, 1)):
+            for i in range(2):
+                load_x(c, u, slice(i * 768, (i + 1) * 768))
+        for g in groups:
+            rows = w[g[0] : g[0] + len(g)].rearrange("e (c p j) n -> p (e c) (j n)", c=2, j=4)
+            nc.sync.dma_start(out=ws[g][:], in_=rows)
+            if g[0] == 0:
+                nc.sync.dma_start(out=gates[:], in_=gate)
+        nc.scalar.dma_start(out=bias[:], in_=b)
+
+        def cast_x(c, u, i):
+            t0, t1 = i * 512, (i + 1) * 512
+            o = xp[c][:, u, 2 * t0 : 2 * t1].rearrange("p (t j) -> p t j", j=2)
+            src = xs[c][u][:, :, t0:t1].rearrange("p j t -> p t j")
+            (vcopy if (c, u, i) in X_ON_VECTOR else scopy)(o, src)
+
+        def gather(c, u):
+            nc.vector.tensor_copy(out=xg[:, u, :], in_=xp[c][:, u, :].bitcast(U32).indirect(offsets[:]))
+
+        def inter_x(c, i):
+            t0, t1 = i * 512, (i + 1) * 512
+            if (c, i) in XI_ON_SCALAR:
+                o = xi[c][:, 4 * t0 : 4 * t1].bitcast(F32).rearrange("p (t u) -> p t u", u=2)
+                src = xp[c][:].bitcast(F32)[:, :, t0:t1].rearrange("p u t -> p t u")
+                scopy(o, src)
+            else:
+                o = xi[c][:, 4 * t0 : 4 * t1].bitcast(I32).rearrange("p (t u) -> p t u", u=2)
+                src = xp[c][:].bitcast(I32)[:, :, t0:t1].rearrange("p u t -> p t u")
+                vcopy(o, src)
+
+        def quant_x(c, i):
+            t0, t1 = i * 512, (i + 1) * 512
+            nc.vector.quantize_mx(out=xq[c][:, t0:t1].bitcast(FP8X4), scales=xsc[c][:, t0:t1], in_=xi[c][:, 4 * t0 : 4 * t1])
+
+        def inter_g(c, i):
+            t0, t1 = i * 512, (i + 1) * 512
+            o = gi[c][:, 4 * t0 : 4 * t1].bitcast(I32).rearrange("p (t u) -> p t u", u=2)
+            src = xg[:].bitcast(I32)[:, :, t0:t1].rearrange("p u t -> p t u")
+            vcopy(o, src)
+
+        def quant_g(c, i):
+            t0, t1 = i * 512, (i + 1) * 512
+            nc.vector.quantize_mx(out=gq[c][:, t0:t1].bitcast(FP8X4), scales=gsc[c][:, t0:t1], in_=gi[c][:, 4 * t0 : 4 * t1])
+
+        def cast_w(g, k):
+            o = wb[g][:, k * 1024 : (k + 1) * 1024].rearrange("p (c n j) -> p c n j", c=2, j=4)
+            src = ws[g][:, 2 * k : 2 * k + 2, :].rearrange("p c (j n) -> p c n j", j=4)
+            (vcopy if g[k] in W_ON_VECTOR else scopy)(o, src)
+
+        def quant_w(g):
+            nc.vector.quantize_mx(out=wq[g][:].bitcast(FP8X4), scales=wsc[g][:], in_=wb[g][:])
+
+        def mm(dst, g, k, codes, scales, cols):
+            for c in range(2):
+                wc = slice((2 * k + c) * 128, (2 * k + c + 1) * 128)
+                nc.tensor.matmul_mx(
+                    out=dst,
+                    lhsT=wq[g][:, wc].bitcast(FP8X4),
+                    lhsT_scale=wsc[g][:, wc],
+                    rhs=codes[c][:, cols].bitcast(FP8X4),
+                    rhs_scale=scales[c][:, cols],
+                    start=(c == 0),
+                    stop=(c == 1),
+                )
+
+        for c in range(2):
+            for u in range(2):
+                for i in range(3):
+                    cast_x(c, u, i)
+                gather(c, u)
+            inter_g(c, 0)
+            inter_g(c, 1)
+            inter_x(c, 0)
+            quant_g(c, 0)
+            quant_g(c, 1)
+            inter_x(c, 1)
+            quant_x(c, 0)
+            inter_x(c, 2)
+            quant_x(c, 1)
+            quant_x(c, 2)
+
+        g8 = groups[0]
+        cast_w(g8, 0)
+        quant_w(g8)
+        for i in range(3):
+            mm(ps[i][:], g8, 0, xq, xsc, slice(i * 512, (i + 1) * 512))
+            nc.scalar.activation(out=ys[:, i * 512 : (i + 1) * 512], in_=ps[i][:], func=GELU, bias=bias[:, 8:9])
+        for q, g in enumerate(groups[1:]):
+            cast_w(g, 0)
+            cast_w(g, 1)
+            quant_w(g)
+            for k in range(2):
+                e = g[k]
+                mm(pr[q][:, k * N : (k + 1) * N], g, k, gq, gsc, slice(e * C, (e + 1) * C))
+                nc.scalar.activation(out=y[:, e * C : (e + 1) * C], in_=pr[q][:, k * N : (k + 1) * N], func=GELU, bias=bias[:, e : e + 1])
+            s0, s1 = q * 256, (q + 1) * 256
+            nc.vector.tensor_tensor(z[:].indirect(offsets[:, s0 // 16 : s1 // 16]), y[:, s0:s1], gates[:, s0:s1], MULT)
+        for i in range(3):
+            cols = slice(i * 512, (i + 1) * 512)
+            nc.vector.tensor_add(ys[:, cols], ys[:, cols], z[:, cols])
+            nc.sync.dma_start(out=out[:, cols], in_=ys[:, cols])

@@ -9,27 +9,40 @@ U8 = mybir.dt.uint8
 FP8X4 = mybir.dt.float8_e4m3fn_x4
 GELU = mybir.ActivationFunctionType.Gelu_apprx_tanh
 MULT = mybir.AluOpType.mult
+ADD = mybir.AluOpType.add
 
 P = 128
 K, T, E, C, N = 1024, 1536, 8, 128, 128
 S = E * C
+SHARED = E
 FLOPS = 2 * K * N * (T + S)
 PASSES = 2
-TC = 512
+K_PASS = K // PASSES
+PAIR_ROWS = 2
+CHUNK = 512
+TOKEN_CHUNKS = T // CHUNK
+SLOT_CHUNKS = S // CHUNK
+GROUPS = ((0, 1), (2, 3), (4, 5), (6, 7), (SHARED,))
 
-X_ON_VECTOR = {(0, 0, 0), (0, 0, 1), (0, 1, 0), (0, 1, 1)}
-W_ON_VECTOR = {8}
-XI_ON_SCALAR = {(1, 2)}
+CAST_X = (("VVV", "GSS"), ("SGV", "SSG"))
+JOIN_TOKENS = ("VVS", "VSS")
+JOIN_SLOTS = ("VS", "VS")
+CAST_W = "SGSSSVSSS"
 
 
 def tile_moe_shr_lin_gelu_kernel(tc, xT, w, b, gate, offs, out):
     nc = tc.nc
 
-    def vcopy(o, i):
-        nc.vector.tensor_copy(out=o, in_=i)
+    def chunk(i):
+        return slice(i * CHUNK, (i + 1) * CHUNK)
 
-    def scopy(o, i):
-        nc.scalar.copy(out=o, in_=i)
+    def copy(engine, dst, src):
+        if engine == "V":
+            nc.vector.tensor_copy(out=dst, in_=src)
+        elif engine == "S":
+            nc.scalar.copy(out=dst, in_=src)
+        else:
+            nc.gpsimd.tensor_scalar(out=dst, in0=src, scalar1=1.0, scalar2=0.0, op0=MULT, op1=ADD)
 
     with (
         tc.tile_pool(name="keep", bufs=1) as keep,
@@ -38,142 +51,136 @@ def tile_moe_shr_lin_gelu_kernel(tc, xT, w, b, gate, offs, out):
         offsets = keep.tile([P, S // 16], U16, name="offsets")
         bias = keep.tile([P, E + 1], F32, name="bias")
         gates = keep.tile([P, S], F32, name="gates")
-        xs = [[keep.tile([P, 2, T], F32, name=f"xs{c}{u}") for u in range(2)] for c in range(2)]
-        xp = [keep.tile([P, 2, 2 * T], BF16, name=f"xp{c}", align_bytes=64) for c in range(2)]
-        xi = [keep.tile([P, 4 * T], BF16, name=f"xi{c}", align_bytes=64) for c in range(2)]
-        xg = keep.tile([P, 2, S], U32, name="xg", align_bytes=64)
-        gi = [keep.tile([P, 4 * S], BF16, name=f"gi{c}", align_bytes=64) for c in range(2)]
-        xq = [keep.tile([P, T], U32, name=f"xq{c}", align_bytes=64) for c in range(2)]
-        xsc = [keep.tile([P, T], U8, name=f"xsc{c}", align_bytes=64) for c in range(2)]
-        gq = [keep.tile([P, S], U32, name=f"gq{c}", align_bytes=64) for c in range(2)]
-        gsc = [keep.tile([P, S], U8, name=f"gsc{c}", align_bytes=64) for c in range(2)]
-        groups = [(8,), (0, 1), (2, 3), (4, 5), (6, 7)]
-        ws = {}
-        wb = {}
-        wq = {}
-        wsc = {}
-        for g in groups:
-            n = len(g) * 2
-            ws[g] = keep.tile([P, n, 512], F32, name=f"ws{g[0]}")
-            wb[g] = keep.tile([P, n * 512], BF16, name=f"wb{g[0]}", align_bytes=64)
-            wq[g] = keep.tile([P, n * 128], U32, name=f"wq{g[0]}", align_bytes=64)
-            wsc[g] = keep.tile([P, n * 128], U8, name=f"wsc{g[0]}", align_bytes=64)
-        ys = keep.tile([P, T], F32, name="ys")
-        y = keep.tile([P, S], F32, name="y")
-        z = keep.tile([P, T], F32, name="z")
-        dummy = keep.tile([P, 8], F32, name="dummy")
-        ps = [psum.tile([P, TC], F32, name=f"ps{i}") for i in range(3)]
-        pr = [psum.tile([P, 2 * N], F32, name=f"pr{i}") for i in range(4)]
 
-        nc.vector.memset(dummy[:], 0.0)
-        nc.scalar.activation(out=dummy[:, 4:5], in_=dummy[:, 0:1], func=GELU)
-        nc.gpsimd.memset(z[:], 0.0)
+        x_raw = [[keep.tile([P, 2, T], F32, name=f"x_raw{c}{u}") for u in range(PAIR_ROWS)] for c in range(PASSES)]
+        x_pairs = [keep.tile([P, PAIR_ROWS, 2 * T], BF16, name=f"x_pairs{c}", align_bytes=64) for c in range(PASSES)]
+        tokens = [keep.tile([P, 4 * T], BF16, name=f"tokens{c}", align_bytes=64) for c in range(PASSES)]
+        token_codes = [keep.tile([P, T], U32, name=f"token_codes{c}", align_bytes=64) for c in range(PASSES)]
+        token_scales = [keep.tile([P, T], U8, name=f"token_scales{c}", align_bytes=64) for c in range(PASSES)]
+        gathered = keep.tile([P, PAIR_ROWS, S], U32, name="gathered", align_bytes=64)
+        slots = [keep.tile([P, 4 * S], BF16, name=f"slots{c}", align_bytes=64) for c in range(PASSES)]
+        slot_codes = [keep.tile([P, S], U32, name=f"slot_codes{c}", align_bytes=64) for c in range(PASSES)]
+        slot_scales = [keep.tile([P, S], U8, name=f"slot_scales{c}", align_bytes=64) for c in range(PASSES)]
 
-        def load_x(c, u, cols):
-            rows = xT[c * 512 : (c + 1) * 512, cols].rearrange("(p u j) t -> p u j t", u=2, j=2)
-            nc.sync.dma_start(out=xs[c][u][:, :, cols], in_=rows[:, u])
+        w_raw = [keep.tile([P, PASSES * len(m), 4 * N], F32, name=f"w_raw{g}") for g, m in enumerate(GROUPS)]
+        w_grouped = [keep.tile([P, PASSES * len(m) * 4 * N], BF16, name=f"w_grouped{g}", align_bytes=64) for g, m in enumerate(GROUPS)]
+        w_codes = [keep.tile([P, PASSES * len(m) * N], U32, name=f"w_codes{g}", align_bytes=64) for g, m in enumerate(GROUPS)]
+        w_scales = [keep.tile([P, PASSES * len(m) * N], U8, name=f"w_scales{g}", align_bytes=64) for g, m in enumerate(GROUPS)]
 
-        for i in range(3):
-            load_x(0, 0, slice(i * 512, (i + 1) * 512))
+        result = keep.tile([P, T], F32, name="result")
+        routed = keep.tile([P, S], F32, name="routed")
+        scattered = keep.tile([P, T], F32, name="scattered")
+        warm = keep.tile([P, 8], F32, name="warm")
+        shared_sums = [psum.tile([P, CHUNK], F32, name=f"shared_sums{i}") for i in range(TOKEN_CHUNKS)]
+        routed_sums = [psum.tile([P, 2 * C], F32, name=f"routed_sums{g}") for g in range(E // 2)]
+
+        nc.vector.memset(warm[:], 0.0)
+        nc.scalar.activation(out=warm[:, 4:5], in_=warm[:, 0:1], func=GELU)
+        nc.gpsimd.memset(scattered[:], 0.0)
+
+        def load_x(c, u):
+            rows = xT[c * K_PASS : (c + 1) * K_PASS, :].rearrange("(p u j) t -> p u j t", u=PAIR_ROWS, j=2)
+            for i in range(TOKEN_CHUNKS):
+                nc.sync.dma_start(out=x_raw[c][u][:, :, chunk(i)], in_=rows[:, u, :, chunk(i)])
+
+        def load_w(g):
+            members = w[GROUPS[g][0] : GROUPS[g][-1] + 1]
+            nc.sync.dma_start(out=w_raw[g][:], in_=members.rearrange("e (c p t) n -> p (e c) (t n)", c=PASSES, t=4))
+
+        load_x(0, 0)
         nc.sync.dma_start(offsets[:], offs)
-        for c, u in ((0, 1), (1, 0), (1, 1)):
-            for i in range(2):
-                load_x(c, u, slice(i * 768, (i + 1) * 768))
-        for g in groups:
-            rows = w[g[0] : g[0] + len(g)].rearrange("e (c p j) n -> p (e c) (j n)", c=2, j=4)
-            nc.sync.dma_start(out=ws[g][:], in_=rows)
-            if g[0] == 0:
-                nc.sync.dma_start(out=gates[:], in_=gate)
+        load_x(0, 1)
+        load_x(1, 0)
+        load_x(1, 1)
+        load_w(0)
+        load_w(1)
+        nc.sync.dma_start(out=gates[:], in_=gate)
+        for g in range(2, len(GROUPS)):
+            load_w(g)
         nc.scalar.dma_start(out=bias[:], in_=b)
 
-        def cast_x(c, u, i):
-            t0, t1 = i * 512, (i + 1) * 512
-            o = xp[c][:, u, 2 * t0 : 2 * t1].rearrange("p (t j) -> p t j", j=2)
-            src = xs[c][u][:, :, t0:t1].rearrange("p j t -> p t j")
-            (vcopy if (c, u, i) in X_ON_VECTOR else scopy)(o, src)
+        def cast_x(c, u):
+            for i, engine in enumerate(CAST_X[c][u]):
+                dst = x_pairs[c][:, u, 2 * i * CHUNK : 2 * (i + 1) * CHUNK].rearrange("p (t j) -> p t j", j=2)
+                copy(engine, dst, x_raw[c][u][:, :, chunk(i)].rearrange("p j t -> p t j"))
 
         def gather(c, u):
-            nc.vector.tensor_copy(out=xg[:, u, :], in_=xp[c][:, u, :].bitcast(U32).indirect(offsets[:]))
+            nc.vector.tensor_copy(out=gathered[:, u, :], in_=x_pairs[c][:, u, :].bitcast(U32).indirect(offsets[:]))
 
-        def inter_x(c, i):
-            t0, t1 = i * 512, (i + 1) * 512
-            if (c, i) in XI_ON_SCALAR:
-                o = xi[c][:, 4 * t0 : 4 * t1].bitcast(F32).rearrange("p (t u) -> p t u", u=2)
-                src = xp[c][:].bitcast(F32)[:, :, t0:t1].rearrange("p u t -> p t u")
-                scopy(o, src)
-            else:
-                o = xi[c][:, 4 * t0 : 4 * t1].bitcast(I32).rearrange("p (t u) -> p t u", u=2)
-                src = xp[c][:].bitcast(I32)[:, :, t0:t1].rearrange("p u t -> p t u")
-                vcopy(o, src)
+        def join(engine, dst, pairs, i):
+            view = I32 if engine == "V" else F32
+            words = dst[:, 4 * i * CHUNK : 4 * (i + 1) * CHUNK].bitcast(view).rearrange("p (t u) -> p t u", u=PAIR_ROWS)
+            copy(engine, words, pairs.bitcast(view)[:, :, chunk(i)].rearrange("p u t -> p t u"))
 
-        def quant_x(c, i):
-            t0, t1 = i * 512, (i + 1) * 512
-            nc.vector.quantize_mx(out=xq[c][:, t0:t1].bitcast(FP8X4), scales=xsc[c][:, t0:t1], in_=xi[c][:, 4 * t0 : 4 * t1])
+        def quantise(codes, scales, grouped):
+            nc.vector.quantize_mx(out=codes.bitcast(FP8X4), scales=scales, in_=grouped)
 
-        def inter_g(c, i):
-            t0, t1 = i * 512, (i + 1) * 512
-            o = gi[c][:, 4 * t0 : 4 * t1].bitcast(I32).rearrange("p (t u) -> p t u", u=2)
-            src = xg[:].bitcast(I32)[:, :, t0:t1].rearrange("p u t -> p t u")
-            vcopy(o, src)
+        def prepare_slots(c):
+            for i, engine in enumerate(JOIN_SLOTS[c]):
+                join(engine, slots[c], gathered[:], i)
+            quantise(slot_codes[c][:], slot_scales[c][:], slots[c][:])
 
-        def quant_g(c, i):
-            t0, t1 = i * 512, (i + 1) * 512
-            nc.vector.quantize_mx(out=gq[c][:, t0:t1].bitcast(FP8X4), scales=gsc[c][:, t0:t1], in_=gi[c][:, 4 * t0 : 4 * t1])
+        def prepare_tokens(c):
+            for i, engine in enumerate(JOIN_TOKENS[c]):
+                join(engine, tokens[c], x_pairs[c][:], i)
+            for i in range(TOKEN_CHUNKS):
+                quantise(token_codes[c][:, chunk(i)], token_scales[c][:, chunk(i)], tokens[c][:, 4 * i * CHUNK : 4 * (i + 1) * CHUNK])
 
-        def cast_w(g, k):
-            o = wb[g][:, k * 1024 : (k + 1) * 1024].rearrange("p (c n j) -> p c n j", c=2, j=4)
-            src = ws[g][:, 2 * k : 2 * k + 2, :].rearrange("p c (j n) -> p c n j", j=4)
-            (vcopy if g[k] in W_ON_VECTOR else scopy)(o, src)
+        def prepare_w(g):
+            for i, e in enumerate(GROUPS[g]):
+                if CAST_W[e] == "S":
+                    for h in range(PASSES * i, PASSES * (i + 1)):
+                        dst = w_grouped[g][:, 4 * N * h : 4 * N * (h + 1)].rearrange("p (n m t) -> p n t m", m=4, t=4)
+                        copy("S", dst, w_raw[g][:, h, :].rearrange("p (t n m) -> p n t m", t=4, m=4))
+                else:
+                    dst = w_grouped[g][:, 4 * N * PASSES * i : 4 * N * PASSES * (i + 1)].rearrange("p (h n t) -> p h n t", n=N, t=4)
+                    copy(CAST_W[e], dst, w_raw[g][:, PASSES * i : PASSES * (i + 1), :].rearrange("p h (t n) -> p h n t", t=4))
+            quantise(w_codes[g][:], w_scales[g][:], w_grouped[g][:])
 
-        def quant_w(g):
-            nc.vector.quantize_mx(out=wq[g][:].bitcast(FP8X4), scales=wsc[g][:], in_=wb[g][:])
-
-        def mm(dst, g, k, codes, scales, cols):
-            for c in range(2):
-                wc = slice((2 * k + c) * 128, (2 * k + c + 1) * 128)
+        def multiply(sums, g, i, codes, scales, columns):
+            for c in range(PASSES):
+                block = slice(N * (PASSES * i + c), N * (PASSES * i + c + 1))
                 nc.tensor.matmul_mx(
-                    out=dst,
-                    lhsT=wq[g][:, wc].bitcast(FP8X4),
-                    lhsT_scale=wsc[g][:, wc],
-                    rhs=codes[c][:, cols].bitcast(FP8X4),
-                    rhs_scale=scales[c][:, cols],
+                    out=sums,
+                    lhsT=w_codes[g][:, block].bitcast(FP8X4),
+                    lhsT_scale=w_scales[g][:, block],
+                    rhs=codes[c][:, columns].bitcast(FP8X4),
+                    rhs_scale=scales[c][:, columns],
                     start=(c == 0),
-                    stop=(c == 1),
+                    stop=(c == PASSES - 1),
                 )
 
-        for c in range(2):
-            for u in range(2):
-                for i in range(3):
-                    cast_x(c, u, i)
-                gather(c, u)
-            inter_g(c, 0)
-            inter_g(c, 1)
-            inter_x(c, 0)
-            quant_g(c, 0)
-            quant_g(c, 1)
-            inter_x(c, 1)
-            quant_x(c, 0)
-            inter_x(c, 2)
-            quant_x(c, 1)
-            quant_x(c, 2)
+        def finish_routed(g):
+            for i, e in enumerate(GROUPS[g]):
+                own = slice(e * C, (e + 1) * C)
+                sums = routed_sums[g][:, i * C : (i + 1) * C]
+                multiply(sums, g, i, slot_codes, slot_scales, own)
+                nc.scalar.activation(out=routed[:, own], in_=sums, func=GELU, bias=bias[:, e : e + 1])
+            first, last = GROUPS[g][0] * C, (GROUPS[g][-1] + 1) * C
+            nc.vector.tensor_tensor(routed[:, first:last], routed[:, first:last], gates[:, first:last], MULT)
+            window = scattered[:].indirect(offsets[:, first // 16 : last // 16])
+            nc.vector.tensor_copy(out=window, in_=routed[:, first:last])
 
-        g8 = groups[0]
-        cast_w(g8, 0)
-        quant_w(g8)
-        for i in range(3):
-            mm(ps[i][:], g8, 0, xq, xsc, slice(i * 512, (i + 1) * 512))
-            nc.scalar.activation(out=ys[:, i * 512 : (i + 1) * 512], in_=ps[i][:], func=GELU, bias=bias[:, 8:9])
-        for q, g in enumerate(groups[1:]):
-            cast_w(g, 0)
-            cast_w(g, 1)
-            quant_w(g)
-            for k in range(2):
-                e = g[k]
-                mm(pr[q][:, k * N : (k + 1) * N], g, k, gq, gsc, slice(e * C, (e + 1) * C))
-                nc.scalar.activation(out=y[:, e * C : (e + 1) * C], in_=pr[q][:, k * N : (k + 1) * N], func=GELU, bias=bias[:, e : e + 1])
-            s0, s1 = q * 256, (q + 1) * 256
-            nc.vector.tensor_tensor(z[:].indirect(offsets[:, s0 // 16 : s1 // 16]), y[:, s0:s1], gates[:, s0:s1], MULT)
-        for i in range(3):
-            cols = slice(i * 512, (i + 1) * 512)
-            nc.vector.tensor_add(ys[:, cols], ys[:, cols], z[:, cols])
-            nc.sync.dma_start(out=out[:, cols], in_=ys[:, cols])
+        for c in range(PASSES):
+            for u in range(PAIR_ROWS):
+                cast_x(c, u)
+                gather(c, u)
+            if c == PASSES - 1:
+                prepare_w(0)
+            prepare_slots(c)
+        prepare_w(1)
+        finish_routed(0)
+        finish_routed(1)
+        for g in (2, 3):
+            prepare_w(g)
+            finish_routed(g)
+        for c in range(PASSES):
+            prepare_tokens(c)
+        shared_group = len(GROUPS) - 1
+        prepare_w(shared_group)
+        for i in range(TOKEN_CHUNKS):
+            multiply(shared_sums[i][:], shared_group, 0, token_codes, token_scales, chunk(i))
+            nc.scalar.activation(out=result[:, chunk(i)], in_=shared_sums[i][:], func=GELU, bias=bias[:, SHARED : SHARED + 1])
+        for i in range(TOKEN_CHUNKS):
+            nc.vector.tensor_add(result[:, chunk(i)], result[:, chunk(i)], scattered[:, chunk(i)])
+            nc.sync.dma_start(out=out[:, chunk(i)], in_=result[:, chunk(i)])

@@ -9,7 +9,6 @@ U8 = mybir.dt.uint8
 FP8X4 = mybir.dt.float8_e4m3fn_x4
 GELU = mybir.ActivationFunctionType.Gelu_apprx_tanh
 MULT = mybir.AluOpType.mult
-ADD = mybir.AluOpType.add
 
 P = 128
 K, T, E, C, N = 1024, 1536, 8, 128, 128
@@ -22,12 +21,37 @@ PAIR_ROWS = 2
 CHUNK = 512
 TOKEN_CHUNKS = T // CHUNK
 SLOT_CHUNKS = S // CHUNK
+EDGES = (0, 512, 1024, T)
+FIRST_EDGES = (0, 640, 1280, T)
+STORE_EDGES = (0, 640, 1280, T)
 GROUPS = ((0, 1), (2, 3), (4, 5), (6, 7), (SHARED,))
 
-CAST_X = (("VVV", "GSS"), ("SGV", "SSG"))
-JOIN_TOKENS = ("VVS", "VSS")
-JOIN_SLOTS = ("VS", "VS")
-CAST_W = "SGSSSVSSS"
+CAST_X = (("SVV", "VSS"), ("SSS", "SSS"))
+JOIN_TOKENS = ("VSV", "SSS")
+JOIN_SLOTS = ("VV", "SV")
+CAST_W = "SSSVSSSVV"
+
+LOADS = (
+    ("x", 0, 0, 0), ("x", 0, 0, 1), ("x", 0, 0, 2), ("offs",), ("x", 0, 1, 1), ("x", 0, 1, 0), ("x", 0, 1, 2),
+    ("x", 1, 0, 1), ("x", 1, 1, 2), ("x", 1, 0, 0), ("x", 1, 0, 2), ("x", 1, 1, 0), ("x", 1, 1, 1), ("w", 0),
+    ("w", 2), ("w", 1), ("w", 3), ("w", 4), ("gate",),
+)
+
+ORDER = (
+    ("cast_x", 0, 0, 1), ("cast_x", 0, 1, 1), ("cast_x", 1, 1, 2), ("cast_x", 1, 0, 2), ("cast_x", 0, 1, 0),
+    ("cast_x", 0, 1, 2), ("cast_x", 0, 0, 2), ("cast_w", 7), ("cast_w", 3), ("cast_x", 0, 0, 0), ("cast_x", 1, 1, 1),
+    ("cast_x", 1, 0, 1), ("gather", 0, 0), ("cast_w", 5), ("cast_w", 2), ("cast_w", 1), ("gather", 0, 1),
+    ("join_tokens", 0, 1), ("join_slots", 0, 1), ("join_tokens", 0, 0), ("quantise_tokens", 0, 0),
+    ("cast_x", 1, 0, 0), ("quantise_w", 1), ("join_tokens", 0, 2), ("cast_x", 1, 1, 0), ("cast_w", 0),
+    ("quantise_tokens", 0, 1), ("join_tokens", 1, 2), ("join_slots", 0, 0), ("quantise_tokens", 1, 2), ("cast_w", 8),
+    ("gather", 1, 0), ("gather", 1, 1), ("join_slots", 1, 0), ("cast_w", 4), ("quantise_w", 0), ("join_slots", 1, 1),
+    ("quantise_slots", 0), ("quantise_slots", 1), ("multiply_routed", 1), ("quantise_tokens", 0, 2),
+    ("quantise_w", 2), ("multiply_routed", 0), ("join_tokens", 1, 0), ("scatter", 0), ("join_tokens", 1, 1),
+    ("quantise_tokens", 1, 1), ("quantise_w", 4), ("cast_w", 6), ("multiply_shared", 1), ("scatter", 1),
+    ("multiply_routed", 2), ("quantise_w", 3), ("multiply_routed", 3), ("scatter", 2), ("quantise_tokens", 1, 0),
+    ("multiply_shared", 2), ("scatter", 3), ("add_and_store", 1), ("multiply_shared", 0), ("add_and_store", 0),
+    ("add_and_store", 2),
+)
 
 
 def tile_moe_shr_lin_gelu_kernel(tc, xT, w, b, gate, offs, out):
@@ -36,13 +60,15 @@ def tile_moe_shr_lin_gelu_kernel(tc, xT, w, b, gate, offs, out):
     def chunk(i):
         return slice(i * CHUNK, (i + 1) * CHUNK)
 
+    def raw_piece(c, u, i):
+        edges = FIRST_EDGES if (c, u) == (0, 0) else EDGES
+        return slice(edges[i], edges[i + 1])
+
     def copy(engine, dst, src):
         if engine == "V":
             nc.vector.tensor_copy(out=dst, in_=src)
-        elif engine == "S":
-            nc.scalar.copy(out=dst, in_=src)
         else:
-            nc.gpsimd.tensor_scalar(out=dst, in0=src, scalar1=1.0, scalar2=0.0, op0=MULT, op1=ADD)
+            nc.scalar.copy(out=dst, in_=src)
 
     with (
         tc.tile_pool(name="keep", bufs=1) as keep,
@@ -78,31 +104,30 @@ def tile_moe_shr_lin_gelu_kernel(tc, xT, w, b, gate, offs, out):
         nc.scalar.activation(out=warm[:, 4:5], in_=warm[:, 0:1], func=GELU)
         nc.gpsimd.memset(scattered[:], 0.0)
 
-        def load_x(c, u):
-            rows = xT[c * K_PASS : (c + 1) * K_PASS, :].rearrange("(p u j) t -> p u j t", u=PAIR_ROWS, j=2)
-            for i in range(TOKEN_CHUNKS):
-                nc.sync.dma_start(out=x_raw[c][u][:, :, chunk(i)], in_=rows[:, u, :, chunk(i)])
+        def load_x(c, u, i):
+            piece = raw_piece(c, u, i)
+            rows = xT[c * K_PASS : (c + 1) * K_PASS, piece].rearrange("(p u j) t -> p u j t", u=PAIR_ROWS, j=2)
+            nc.sync.dma_start(out=x_raw[c][u][:, :, piece], in_=rows[:, u])
 
         def load_w(g):
             members = w[GROUPS[g][0] : GROUPS[g][-1] + 1]
             nc.sync.dma_start(out=w_raw[g][:], in_=members.rearrange("e (c p t) n -> p (e c) (t n)", c=PASSES, t=4))
 
-        load_x(0, 0)
-        nc.sync.dma_start(offsets[:], offs)
-        load_x(0, 1)
-        load_x(1, 0)
-        load_x(1, 1)
-        load_w(0)
-        load_w(1)
-        nc.sync.dma_start(out=gates[:], in_=gate)
-        for g in range(2, len(GROUPS)):
-            load_w(g)
+        def load_offsets():
+            nc.sync.dma_start(offsets[:], offs)
+
+        def load_gates():
+            nc.sync.dma_start(out=gates[:], in_=gate)
+
+        loaders = {"x": load_x, "w": load_w, "offs": load_offsets, "gate": load_gates}
+        for load in LOADS:
+            loaders[load[0]](*load[1:])
         nc.scalar.dma_start(out=bias[:], in_=b)
 
-        def cast_x(c, u):
-            for i, engine in enumerate(CAST_X[c][u]):
-                dst = x_pairs[c][:, u, 2 * i * CHUNK : 2 * (i + 1) * CHUNK].rearrange("p (t j) -> p t j", j=2)
-                copy(engine, dst, x_raw[c][u][:, :, chunk(i)].rearrange("p j t -> p t j"))
+        def cast_x(c, u, i):
+            piece = raw_piece(c, u, i)
+            dst = x_pairs[c][:, u, 2 * piece.start : 2 * piece.stop].rearrange("p (t j) -> p t j", j=2)
+            copy(CAST_X[c][u][i], dst, x_raw[c][u][:, :, piece].rearrange("p j t -> p t j"))
 
         def gather(c, u):
             nc.vector.tensor_copy(out=gathered[:, u, :], in_=x_pairs[c][:, u, :].bitcast(U32).indirect(offsets[:]))
@@ -115,26 +140,30 @@ def tile_moe_shr_lin_gelu_kernel(tc, xT, w, b, gate, offs, out):
         def quantise(codes, scales, grouped):
             nc.vector.quantize_mx(out=codes.bitcast(FP8X4), scales=scales, in_=grouped)
 
-        def prepare_slots(c):
-            for i, engine in enumerate(JOIN_SLOTS[c]):
-                join(engine, slots[c], gathered[:], i)
+        def join_tokens(c, i):
+            join(JOIN_TOKENS[c][i], tokens[c], x_pairs[c][:], i)
+
+        def join_slots(c, i):
+            join(JOIN_SLOTS[c][i], slots[c], gathered[:], i)
+
+        def quantise_tokens(c, i):
+            quantise(token_codes[c][:, chunk(i)], token_scales[c][:, chunk(i)], tokens[c][:, 4 * i * CHUNK : 4 * (i + 1) * CHUNK])
+
+        def quantise_slots(c):
             quantise(slot_codes[c][:], slot_scales[c][:], slots[c][:])
 
-        def prepare_tokens(c):
-            for i, engine in enumerate(JOIN_TOKENS[c]):
-                join(engine, tokens[c], x_pairs[c][:], i)
-            for i in range(TOKEN_CHUNKS):
-                quantise(token_codes[c][:, chunk(i)], token_scales[c][:, chunk(i)], tokens[c][:, 4 * i * CHUNK : 4 * (i + 1) * CHUNK])
+        def cast_w(e):
+            g = e // 2
+            i = e % 2
+            if CAST_W[e] == "S":
+                for h in range(PASSES * i, PASSES * (i + 1)):
+                    dst = w_grouped[g][:, 4 * N * h : 4 * N * (h + 1)].rearrange("p (n m t) -> p n t m", m=4, t=4)
+                    copy("S", dst, w_raw[g][:, h, :].rearrange("p (t n m) -> p n t m", t=4, m=4))
+            else:
+                dst = w_grouped[g][:, 4 * N * PASSES * i : 4 * N * PASSES * (i + 1)].rearrange("p (h n t) -> p h n t", n=N, t=4)
+                copy("V", dst, w_raw[g][:, PASSES * i : PASSES * (i + 1), :].rearrange("p h (t n) -> p h n t", t=4))
 
-        def prepare_w(g):
-            for i, e in enumerate(GROUPS[g]):
-                if CAST_W[e] == "S":
-                    for h in range(PASSES * i, PASSES * (i + 1)):
-                        dst = w_grouped[g][:, 4 * N * h : 4 * N * (h + 1)].rearrange("p (n m t) -> p n t m", m=4, t=4)
-                        copy("S", dst, w_raw[g][:, h, :].rearrange("p (t n m) -> p n t m", t=4, m=4))
-                else:
-                    dst = w_grouped[g][:, 4 * N * PASSES * i : 4 * N * PASSES * (i + 1)].rearrange("p (h n t) -> p h n t", n=N, t=4)
-                    copy(CAST_W[e], dst, w_raw[g][:, PASSES * i : PASSES * (i + 1), :].rearrange("p h (t n) -> p h n t", t=4))
+        def quantise_w(g):
             quantise(w_codes[g][:], w_scales[g][:], w_grouped[g][:])
 
         def multiply(sums, g, i, codes, scales, columns):
@@ -150,37 +179,40 @@ def tile_moe_shr_lin_gelu_kernel(tc, xT, w, b, gate, offs, out):
                     stop=(c == PASSES - 1),
                 )
 
-        def finish_routed(g):
+        def multiply_routed(g):
             for i, e in enumerate(GROUPS[g]):
                 own = slice(e * C, (e + 1) * C)
                 sums = routed_sums[g][:, i * C : (i + 1) * C]
                 multiply(sums, g, i, slot_codes, slot_scales, own)
                 nc.scalar.activation(out=routed[:, own], in_=sums, func=GELU, bias=bias[:, e : e + 1])
-            first, last = GROUPS[g][0] * C, (GROUPS[g][-1] + 1) * C
-            nc.vector.tensor_tensor(routed[:, first:last], routed[:, first:last], gates[:, first:last], MULT)
-            window = scattered[:].indirect(offsets[:, first // 16 : last // 16])
-            nc.vector.tensor_copy(out=window, in_=routed[:, first:last])
 
-        for c in range(PASSES):
-            for u in range(PAIR_ROWS):
-                cast_x(c, u)
-                gather(c, u)
-            if c == PASSES - 1:
-                prepare_w(0)
-            prepare_slots(c)
-        prepare_w(1)
-        finish_routed(0)
-        finish_routed(1)
-        for g in (2, 3):
-            prepare_w(g)
-            finish_routed(g)
-        for c in range(PASSES):
-            prepare_tokens(c)
-        shared_group = len(GROUPS) - 1
-        prepare_w(shared_group)
-        for i in range(TOKEN_CHUNKS):
-            multiply(shared_sums[i][:], shared_group, 0, token_codes, token_scales, chunk(i))
+        def scatter(g):
+            first, last = GROUPS[g][0] * C, (GROUPS[g][-1] + 1) * C
+            window = scattered[:].indirect(offsets[:, first // 16 : last // 16])
+            nc.vector.tensor_tensor(window, routed[:, first:last], gates[:, first:last], MULT)
+
+        def multiply_shared(i):
+            multiply(shared_sums[i][:], SHARED // 2, 0, token_codes, token_scales, chunk(i))
             nc.scalar.activation(out=result[:, chunk(i)], in_=shared_sums[i][:], func=GELU, bias=bias[:, SHARED : SHARED + 1])
-        for i in range(TOKEN_CHUNKS):
-            nc.vector.tensor_add(result[:, chunk(i)], result[:, chunk(i)], scattered[:, chunk(i)])
-            nc.sync.dma_start(out=out[:, chunk(i)], in_=result[:, chunk(i)])
+
+        def add_and_store(i):
+            columns = slice(STORE_EDGES[i], STORE_EDGES[i + 1])
+            nc.vector.tensor_add(result[:, columns], result[:, columns], scattered[:, columns])
+            nc.sync.dma_start(out=out[:, columns], in_=result[:, columns])
+
+        steps = {
+            "cast_x": cast_x,
+            "gather": gather,
+            "join_tokens": join_tokens,
+            "quantise_tokens": quantise_tokens,
+            "join_slots": join_slots,
+            "quantise_slots": quantise_slots,
+            "cast_w": cast_w,
+            "quantise_w": quantise_w,
+            "multiply_routed": multiply_routed,
+            "scatter": scatter,
+            "multiply_shared": multiply_shared,
+            "add_and_store": add_and_store,
+        }
+        for step in ORDER:
+            steps[step[0]](*step[1:])

import concourse.mybir as mybir

F32 = mybir.dt.float32
BF16 = mybir.dt.bfloat16
U32 = mybir.dt.uint32
I32 = mybir.dt.int32
U16 = mybir.dt.uint16
U8 = mybir.dt.uint8
FP8X4 = mybir.dt.float8_e4m3fn_x4
GELU = mybir.ActivationFunctionType.Gelu_apprx_tanh
MULT = mybir.AluOpType.mult

P = 128
K, T, E, C, N = 1024, 1536, 8, 128, 128
S = E * C
SHARED = E
FLOPS = 2 * K * N * (T + S)
PASSES = 2
K_PASS = K // PASSES
PAIR_ROWS = 2
CHUNK = 512
TOKEN_CHUNKS = T // CHUNK
SLOT_CHUNKS = S // CHUNK
EDGES = (0, 512, 1024, T)
FIRST_EDGES = (0, 640, 1280, T)
STORE_EDGES = (0, 640, 1280, T)
GROUPS = ((0, 1), (2, 3), (4, 5), (6, 7), (SHARED,))

CAST_X = (("SVV", "VSS"), ("SSS", "SSS"))
JOIN_TOKENS = ("VSV", "SSS")
JOIN_SLOTS = ("VV", "SV")
CAST_W = "SSSVSSSVV"

LOADS = (
    ("x", 0, 0, 0), ("x", 0, 0, 1), ("x", 0, 0, 2), ("offs",), ("x", 0, 1, 1), ("x", 0, 1, 0), ("x", 0, 1, 2),
    ("x", 1, 0, 1), ("x", 1, 1, 2), ("x", 1, 0, 0), ("x", 1, 0, 2), ("x", 1, 1, 0), ("x", 1, 1, 1), ("w", 0),
    ("w", 2), ("w", 1), ("w", 3), ("w", 4), ("gate",),
)

ORDER = (
    ("cast_x", 0, 0, 1), ("cast_x", 0, 1, 1), ("cast_x", 1, 1, 2), ("cast_x", 1, 0, 2), ("cast_x", 0, 1, 0),
    ("cast_x", 0, 1, 2), ("cast_x", 0, 0, 2), ("cast_w", 7), ("cast_w", 3), ("cast_x", 0, 0, 0), ("cast_x", 1, 1, 1),
    ("cast_x", 1, 0, 1), ("gather", 0, 0), ("cast_w", 5), ("cast_w", 2), ("cast_w", 1), ("gather", 0, 1),
    ("join_tokens", 0, 1), ("join_slots", 0, 1), ("join_tokens", 0, 0), ("quantise_tokens", 0, 0),
    ("cast_x", 1, 0, 0), ("quantise_w", 1), ("join_tokens", 0, 2), ("cast_x", 1, 1, 0), ("cast_w", 0),
    ("quantise_tokens", 0, 1), ("join_tokens", 1, 2), ("join_slots", 0, 0), ("quantise_tokens", 1, 2), ("cast_w", 8),
    ("gather", 1, 0), ("gather", 1, 1), ("join_slots", 1, 0), ("cast_w", 4), ("quantise_w", 0), ("join_slots", 1, 1),
    ("quantise_slots", 0), ("quantise_slots", 1), ("multiply_routed", 1), ("quantise_tokens", 0, 2),
    ("quantise_w", 2), ("multiply_routed", 0), ("join_tokens", 1, 0), ("scatter", 0), ("join_tokens", 1, 1),
    ("quantise_tokens", 1, 1), ("quantise_w", 4), ("cast_w", 6), ("multiply_shared", 1), ("scatter", 1),
    ("multiply_routed", 2), ("quantise_w", 3), ("multiply_routed", 3), ("scatter", 2), ("quantise_tokens", 1, 0),
    ("multiply_shared", 2), ("scatter", 3), ("add_and_store", 1), ("multiply_shared", 0), ("add_and_store", 0),
    ("add_and_store", 2),
)


def tile_moe_shr_lin_gelu_kernel(tc, xT, w, b, gate, offs, out):
    nc = tc.nc

    def chunk(i):
        return slice(i * CHUNK, (i + 1) * CHUNK)

    def raw_piece(c, u, i):
        edges = FIRST_EDGES if (c, u) == (0, 0) else EDGES
        return slice(edges[i], edges[i + 1])

    def copy(engine, dst, src):
        if engine == "V":
            nc.vector.tensor_copy(out=dst, in_=src)
        else:
            nc.scalar.copy(out=dst, in_=src)

    with (
        tc.tile_pool(name="keep", bufs=1) as keep,
        tc.psum_pool(name="psum", bufs=1) as psum,
    ):
        offsets = keep.tile([P, S // 16], U16, name="offsets")
        bias = keep.tile([P, E + 1], F32, name="bias")
        gates = keep.tile([P, S], F32, name="gates")

        x_raw = [[keep.tile([P, 2, T], F32, name=f"x_raw{c}{u}") for u in range(PAIR_ROWS)] for c in range(PASSES)]
        x_pairs = [keep.tile([P, PAIR_ROWS, 2 * T], BF16, name=f"x_pairs{c}", align_bytes=64) for c in range(PASSES)]
        tokens = [keep.tile([P, 4 * T], BF16, name=f"tokens{c}", align_bytes=64) for c in range(PASSES)]
        token_codes = [keep.tile([P, T], U32, name=f"token_codes{c}", align_bytes=64) for c in range(PASSES)]
        token_scales = [keep.tile([P, T], U8, name=f"token_scales{c}", align_bytes=64) for c in range(PASSES)]
        gathered = keep.tile([P, PAIR_ROWS, S], U32, name="gathered", align_bytes=64)
        slots = [keep.tile([P, 4 * S], BF16, name=f"slots{c}", align_bytes=64) for c in range(PASSES)]
        slot_codes = [keep.tile([P, S], U32, name=f"slot_codes{c}", align_bytes=64) for c in range(PASSES)]
        slot_scales = [keep.tile([P, S], U8, name=f"slot_scales{c}", align_bytes=64) for c in range(PASSES)]

        w_raw = [keep.tile([P, PASSES * len(m), 4 * N], F32, name=f"w_raw{g}") for g, m in enumerate(GROUPS)]
        w_grouped = [keep.tile([P, PASSES * len(m) * 4 * N], BF16, name=f"w_grouped{g}", align_bytes=64) for g, m in enumerate(GROUPS)]
        w_codes = [keep.tile([P, PASSES * len(m) * N], U32, name=f"w_codes{g}", align_bytes=64) for g, m in enumerate(GROUPS)]
        w_scales = [keep.tile([P, PASSES * len(m) * N], U8, name=f"w_scales{g}", align_bytes=64) for g, m in enumerate(GROUPS)]

        result = keep.tile([P, T], F32, name="result")
        routed = keep.tile([P, S], F32, name="routed")
        scattered = keep.tile([P, T], F32, name="scattered")
        warm = keep.tile([P, 8], F32, name="warm")
        shared_sums = [psum.tile([P, CHUNK], F32, name=f"shared_sums{i}") for i in range(TOKEN_CHUNKS)]
        routed_sums = [psum.tile([P, 2 * C], F32, name=f"routed_sums{g}") for g in range(E // 2)]

        nc.vector.memset(warm[:], 0.0)
        nc.scalar.activation(out=warm[:, 4:5], in_=warm[:, 0:1], func=GELU)
        nc.gpsimd.memset(scattered[:], 0.0)

        def load_x(c, u, i):
            piece = raw_piece(c, u, i)
            rows = xT[c * K_PASS : (c + 1) * K_PASS, piece].rearrange("(p u j) t -> p u j t", u=PAIR_ROWS, j=2)
            nc.sync.dma_start(out=x_raw[c][u][:, :, piece], in_=rows[:, u])

        def load_w(g):
            members = w[GROUPS[g][0] : GROUPS[g][-1] + 1]
            nc.sync.dma_start(out=w_raw[g][:], in_=members.rearrange("e (c p t) n -> p (e c) (t n)", c=PASSES, t=4))

        def load_offsets():
            nc.sync.dma_start(offsets[:], offs)

        def load_gates():
            nc.sync.dma_start(out=gates[:], in_=gate)

        loaders = {"x": load_x, "w": load_w, "offs": load_offsets, "gate": load_gates}
        for load in LOADS:
            loaders[load[0]](*load[1:])
        nc.scalar.dma_start(out=bias[:], in_=b)

        def cast_x(c, u, i):
            piece = raw_piece(c, u, i)
            dst = x_pairs[c][:, u, 2 * piece.start : 2 * piece.stop].rearrange("p (t j) -> p t j", j=2)
            copy(CAST_X[c][u][i], dst, x_raw[c][u][:, :, piece].rearrange("p j t -> p t j"))

        def gather(c, u):
            nc.vector.tensor_copy(out=gathered[:, u, :], in_=x_pairs[c][:, u, :].bitcast(U32).indirect(offsets[:]))

        def join(engine, dst, pairs, i):
            view = I32 if engine == "V" else F32
            words = dst[:, 4 * i * CHUNK : 4 * (i + 1) * CHUNK].bitcast(view).rearrange("p (t u) -> p t u", u=PAIR_ROWS)
            copy(engine, words, pairs.bitcast(view)[:, :, chunk(i)].rearrange("p u t -> p t u"))

        def quantise(codes, scales, grouped):
            nc.vector.quantize_mx(out=codes.bitcast(FP8X4), scales=scales, in_=grouped)

        def join_tokens(c, i):
            join(JOIN_TOKENS[c][i], tokens[c], x_pairs[c][:], i)

        def join_slots(c, i):
            join(JOIN_SLOTS[c][i], slots[c], gathered[:], i)

        def quantise_tokens(c, i):
            quantise(token_codes[c][:, chunk(i)], token_scales[c][:, chunk(i)], tokens[c][:, 4 * i * CHUNK : 4 * (i + 1) * CHUNK])

        def quantise_slots(c):
            quantise(slot_codes[c][:], slot_scales[c][:], slots[c][:])

        def cast_w(e):
            g = e // 2
            i = e % 2
            if CAST_W[e] == "S":
                for h in range(PASSES * i, PASSES * (i + 1)):
                    dst = w_grouped[g][:, 4 * N * h : 4 * N * (h + 1)].rearrange("p (n m t) -> p n t m", m=4, t=4)
                    copy("S", dst, w_raw[g][:, h, :].rearrange("p (t n m) -> p n t m", t=4, m=4))
            else:
                dst = w_grouped[g][:, 4 * N * PASSES * i : 4 * N * PASSES * (i + 1)].rearrange("p (h n t) -> p h n t", n=N, t=4)
                copy("V", dst, w_raw[g][:, PASSES * i : PASSES * (i + 1), :].rearrange("p h (t n) -> p h n t", t=4))

        def quantise_w(g):
            quantise(w_codes[g][:], w_scales[g][:], w_grouped[g][:])

        def multiply(sums, g, i, codes, scales, columns):
            for c in range(PASSES):
                block = slice(N * (PASSES * i + c), N * (PASSES * i + c + 1))
                nc.tensor.matmul_mx(
                    out=sums,
                    lhsT=w_codes[g][:, block].bitcast(FP8X4),
                    lhsT_scale=w_scales[g][:, block],
                    rhs=codes[c][:, columns].bitcast(FP8X4),
                    rhs_scale=scales[c][:, columns],
                    start=(c == 0),
                    stop=(c == PASSES - 1),
                )

        def multiply_routed(g):
            for i, e in enumerate(GROUPS[g]):
                own = slice(e * C, (e + 1) * C)
                sums = routed_sums[g][:, i * C : (i + 1) * C]
                multiply(sums, g, i, slot_codes, slot_scales, own)
                nc.scalar.activation(out=routed[:, own], in_=sums, func=GELU, bias=bias[:, e : e + 1])

        def scatter(g):
            first, last = GROUPS[g][0] * C, (GROUPS[g][-1] + 1) * C
            window = scattered[:].indirect(offsets[:, first // 16 : last // 16])
            nc.vector.tensor_tensor(window, routed[:, first:last], gates[:, first:last], MULT)

        def multiply_shared(i):
            multiply(shared_sums[i][:], SHARED // 2, 0, token_codes, token_scales, chunk(i))
            nc.scalar.activation(out=result[:, chunk(i)], in_=shared_sums[i][:], func=GELU, bias=bias[:, SHARED : SHARED + 1])

        def add_and_store(i):
            columns = slice(STORE_EDGES[i], STORE_EDGES[i + 1])
            nc.vector.tensor_add(result[:, columns], result[:, columns], scattered[:, columns])
            nc.sync.dma_start(out=out[:, columns], in_=result[:, columns])

        steps = {
            "cast_x": cast_x,
            "gather": gather,
            "join_tokens": join_tokens,
            "quantise_tokens": quantise_tokens,
            "join_slots": join_slots,
            "quantise_slots": quantise_slots,
            "cast_w": cast_w,
            "quantise_w": quantise_w,
            "multiply_routed": multiply_routed,
            "scatter": scatter,
            "multiply_shared": multiply_shared,
            "add_and_store": add_and_store,
        }
        for step in ORDER:
            steps[step[0]](*step[1:])
